import numpy as np
import ml_dtypes


def mxq(x, axis, fmt="e4m3"):
    dtype, down = {"e4m3": (ml_dtypes.float8_e4m3fn, 7), "e5m2": (ml_dtypes.float8_e5m2, 14)}[fmt]
    v = np.moveaxis(np.asarray(x, np.float32).astype(ml_dtypes.bfloat16).astype(np.float64), axis, -1)
    blocks = v.reshape(v.shape[:-1] + (-1, 32))
    amax = np.abs(blocks).max(-1, keepdims=True)
    byte = np.maximum(np.where(amax > 0, np.frexp(amax)[1] - 1 + 127, 0) - down, 1)
    scale = np.exp2(byte - 127.0)
    codes = (blocks / scale).astype(np.float32).astype(dtype).astype(np.float64)
    return np.moveaxis((codes * scale).reshape(v.shape), -1, axis)


WIDE = False


def mx_kscale(k):
    if not WIDE:
        return np.ones(k)
    levels = np.array([10, -10, 5, -5, 0])
    if k % 512:
        return np.exp2(np.random.permutation(np.resize(levels, k // 32))).repeat(32)
    a = np.empty((k // 512, 16))
    for p in range(k // 512):
        a[p, :8] = np.random.permutation(np.resize(levels, 8))
        for g in range(8):
            far = levels[np.abs(levels - a[p, g]) >= 10]
            a[p, g + 8] = far[np.random.randint(len(far))]
    return np.exp2(a.ravel()).repeat(32)


def f64(x):
    return np.asarray(x).astype(np.float64)


def striped(idx):
    return np.tile(idx.reshape(-1, 16).T, (8, 1)).astype(np.uint16)


def unstriped(offs):
    return offs[:16].T.reshape(-1).astype(np.int64)


def pack_weight(w):
    k, n = w.shape
    w = f64(np.asarray(w, np.float32).astype(ml_dtypes.bfloat16)).reshape(k // 32, 32, n)
    amax = np.abs(w).max(1)
    byte = np.clip(np.where(amax > 0, np.frexp(amax)[1] - 1 + 127 - 7, 1), 1, 254)
    scaled = (w * np.exp2(127.0 - byte)[:, None, :]).reshape(k, n).astype(np.float32)
    words = np.ascontiguousarray(scaled.reshape(k // 512, 128, 4, n).transpose(0, 1, 3, 2)).astype(ml_dtypes.float8_e4m3fn).view(np.uint8)
    return words, np.ascontiguousarray(byte.astype(np.uint8).reshape(k // 512, 16, n))


def unpack_weight(words, scales):
    g, p, n, _ = words.shape
    vals = np.ascontiguousarray(words).view(ml_dtypes.float8_e4m3fn).astype(np.float64) * np.repeat(np.exp2(scales.astype(np.float64) - 127.0), 8, axis=1)[..., None]
    return vals.transpose(0, 1, 3, 2).reshape(g * 512, n)


K, T, S, D, N, H = 512, 2048, 512, 2, 256, 512


def setup_inputs():
    n = np.random.standard_normal
    s = mx_kscale(K)[:, None]
    u = mx_kscale(H)
    packed_xT = pack_weight(n((K, T)) * s)
    return {
        "x_words": packed_xT[0],
        "x_scales": packed_xT[1],
        "w1": (n((K, H)) / np.sqrt(K) / s).astype(np.float32),
        "w2": (n((K, H)) / np.sqrt(K) / s).astype(np.float32),
        "unit": (np.random.uniform(0.6, 1.4, (H, 1)) * u[:, None]).astype(np.float32),
        "w3": (n((H, N)) / np.sqrt(H) / u[:, None]).astype(np.float32),
        "offs": striped(np.random.permutation(T)[:S]),
        "riv": striped(np.random.permutation(S)),
    }


def reference(x_words, x_scales, w1, w2, unit, w3, offs, riv):
    xq = unpack_weight(x_words, x_scales)[:, unstriped(offs)]
    hk = mxq(f64(w2), 0, "e4m3").T @ xq
    aff = np.log(np.exp(hk) + 1.0) + 0.2
    pr = mxq(f64(w1), 0, "e4m3").T @ xq
    press = np.log(np.exp(pr) + 1.0)
    kp = np.sqrt(aff * press + 0.02)
    kr = kp[:, unstriped(riv)]
    load = kp / (kp + kr + 1.0)
    mix = load.reshape(len(load), -1, D).sum(axis=2)
    sel = load / (np.repeat(mix, D, axis=1) + 0.2)
    hid = f64(unit) * (load - (0.6 * sel))
    return mxq(f64(w3), 0, "e4m3").T @ mxq(hid, 0, "e4m3")

@@ -1,0 +1,213 @@
+from contextlib import ExitStack
+
+import concourse.mybir as mybir
+
+K, T, S, H, N = 512, 2048, 512, 512, 256
+FLOPS = 2 * K * H * S * 2 + 2 * H * N * S
+
+F32 = mybir.dt.float32
+BF16 = mybir.dt.bfloat16
+I32 = mybir.dt.int32
+U32 = mybir.dt.uint32
+U16 = mybir.dt.uint16
+U8 = mybir.dt.uint8
+FP8X4 = mybir.dt.float8_e4m3fn_x4
+ACT = mybir.ActivationFunctionType
+ALU = mybir.AluOpType
+
+P = 128
+PACK = 4
+CHUNKS = [128,128,128,64,64]
+FLOOR = 2.0 ** -44
+SCALAR_GATHER = [2]
+VECTOR_PLUS = []
+POOL_PROD = []
+
+
+def tile_picked_yadsiso_load_p_kernel(tc, x_words, x_scales, w1, w2, unit, w3, offs, riv, out):
+    nc = tc.nc
+    with ExitStack() as ctx:
+        keep = ctx.enter_context(tc.tile_pool(name="keep", bufs=1))
+        psum = ctx.enter_context(tc.psum_pool(name="psum", bufs=1))
+
+        offs_t = keep.tile([P, S // 16], U16, name="offs_t")
+        riv_t = keep.tile([P, S // 16], U16, name="riv_t")
+        table_words = keep.tile([P, T], I32, name="table_words", align_bytes=64)
+        table_scales = keep.tile([P, T], U8, name="table_scales", align_bytes=64)
+        nc.gpsimd.memset(table_scales[:].bitcast(I32), 0)
+        half = H // 2
+        raw_w2 = keep.tile([P, PACK, H], F32, name="raw_w2")
+        nc.sync.dma_start(raw_w2[:], w2.rearrange("(p j) c -> p j c", j=PACK))
+        for q in range(4):
+            nc.sync.dma_start(table_scales[32 * q : 32 * q + 4, :].bitcast(I32), x_scales[0, 4 * q : 4 * q + 4, :].bitcast(I32))
+        nc.sync.dma_start(offs_t[:], offs)
+        nc.sync.dma_start(table_words[:], x_words[0].rearrange("p n t -> p (n t)").bitcast(I32))
+        raw_w1 = []
+        for h in range(2):
+            raw_w1.append(keep.tile([P, PACK, half], F32, name="raw_w1_%d" % h))
+            nc.sync.dma_start(raw_w1[h][:], w1.rearrange("(p j) c -> p j c", j=PACK)[:, :, h * half : (h + 1) * half])
+        raw_w3 = keep.tile([P, PACK, N], F32, name="raw_w3")
+        nc.sync.dma_start(raw_w3[:], w3.rearrange("(p j) c -> p j c", j=PACK))
+        unit_t = keep.tile([P, PACK], F32, name="unit_t")
+        nc.sync.dma_start(unit_t[:], unit.rearrange("(p t) o -> p (t o)", t=PACK))
+        nc.sync.dma_start(riv_t[:], riv)
+
+        grouped = {name: keep.tile([P, PACK, P, PACK], BF16, name="grouped_" + name, align_bytes=64) for name in ("w2", "w1")}
+        codes = {name: keep.tile([P, H], U32, name="codes_" + name, align_bytes=64) for name in ("w2", "w1")}
+        plane = {name: keep.tile([P, H], U8, name="plane_" + name, align_bytes=64) for name in ("w2", "w1")}
+
+        x_codes = [keep.tile([P, S // 2], U32, name="x_codes_%d" % h, align_bytes=64) for h in range(2)]
+        x_plane = keep.tile([P, S], U8, name="x_plane", align_bytes=64)
+        nc.vector.tensor_copy(x_plane[:], table_scales[:].indirect(offs_t[:]))
+        nc.vector.tensor_scalar(grouped["w2"][:].rearrange("p t m j -> p m j t"), raw_w2[:].rearrange("p j (m t) -> p m j t", t=PACK), -1.0, None, ALU.mult)
+        nc.vector.quantize_mx(codes["w2"][:].bitcast(FP8X4), plane["w2"][:], grouped["w2"][:].rearrange("p t m j -> p (t m j)"))
+        for h in range(2):
+            nc.vector.tensor_copy(x_codes[h][:], table_words[:].bitcast(U32).indirect(offs_t[:, 16 * h : 16 * (h + 1)]))
+
+        U = S // 2
+        ring = keep.tile([P, 22 * U], F32, name="ring")
+
+        def span(u):
+            return ring[:, u * U : (u + 2) * U]
+
+        sig_at = {("w2", 0): 0, ("w2", 1): 2, ("w2", 2): 4, ("w2", 3): 6, ("w1", 0): 8, ("w1", 1): 10, ("w1", 3): 13, ("w1", 2): 17}
+
+        banks = {}
+
+        def first_products(name):
+            for t in range(PACK):
+                cols = slice(t * P, (t + 1) * P)
+                banks[name, t] = psum.tile([P, S], F32, name="bank_%s_%d" % (name, t), tag="bank_%s_%d" % (name, t))
+                for h in range(2):
+                    hc = slice(h * U, (h + 1) * U)
+                    nc.tensor.matmul_mx(banks[name, t][:, hc], codes[name][:, cols].bitcast(FP8X4), plane[name][:, cols],
+                                        x_codes[h][:].bitcast(FP8X4), x_plane[:, hc], start=True, stop=True)
+                nc.scalar.activation(span(sig_at[name, t]), banks[name, t][:], ACT.Sigmoid, scale=1.0 if name == "w2" else -1.0)
+
+        first_products("w2")
+        for h in range(2):
+            nc.vector.tensor_copy(
+                grouped["w1"][:, :, h * 64 : (h + 1) * 64, :].rearrange("p t m j -> p m j t"),
+                raw_w1[h][:].rearrange("p j (m t) -> p m j t", t=PACK),
+            )
+        for t in range(PACK):
+            cols = slice(t * P, (t + 1) * P)
+            nc.vector.quantize_mx(codes["w1"][:, cols].bitcast(FP8X4), plane["w1"][:, cols], grouped["w1"][:, t].rearrange("p m j -> p (m j)"))
+        first_products("w1")
+
+        grouped_w3 = keep.tile([P, N, PACK], BF16, name="grouped_w3", align_bytes=64)
+        nc.vector.tensor_copy(grouped_w3[:].rearrange("p (c i) j -> p c j i", i=4), raw_w3[:].rearrange("p j (c i) -> p c j i", i=4))
+        gain = keep.tile([P, PACK], F32, name="gain")
+        nc.vector.tensor_scalar(gain[:], unit_t[:], -0.6, None, ALU.mult)
+        codes_w3 = keep.tile([P, N], U32, name="codes_w3", align_bytes=64)
+        plane_w3 = keep.tile([P, N], U8, name="plane_w3", align_bytes=64)
+        nc.vector.quantize_mx(codes_w3[:].bitcast(FP8X4), plane_w3[:], grouped_w3[:].rearrange("p c j -> p (c j)"))
+
+        ln_order = [("w1", 3), ("w2", 3), ("w2", 0), ("w1", 0), ("w2", 1), ("w1", 1), ("w2", 2), ("w1", 2)]
+        ln_at = {ln_order[0]: 20, ln_order[1]: 12, ln_order[2]: 14}
+        for i in range(3, 8):
+            ln_at[ln_order[i]] = sig_at[ln_order[i - 2]]
+        shrink = 2.718281828459045 ** -0.2
+        for key in ln_order:
+            s = shrink if key[0] == "w2" else 1.0
+            nc.scalar.activation(span(ln_at[key]), span(sig_at[key]), ACT.Ln, bias=FLOOR * s, scale=s)
+
+        order = [3, 0, 1, 2]
+        prod = {}
+        inv_kp = {order[0]: span(16), order[1]: span(18)}
+        for t in order[2:]:
+            inv_kp[t] = keep.tile([P, S], F32, name="inv_kp_%d" % t)[:]
+        starts = [sum(CHUNKS[:c]) for c in range(len(CHUNKS))]
+        ratio = [keep.tile([P, PACK, n], F32, name="ratio_%d" % c) for c, n in enumerate(CHUNKS)]
+        window = {}
+
+        def product(t):
+            neg_p = keep.tile([P, S], F32, name="neg_p_%d" % t)
+            nc.vector.scalar_tensor_tensor(neg_p[:], banks["w1", t][:], -1.0, span(ln_at["w1", t]), ALU.mult, ALU.min)
+            neg_a = keep.tile([P, S], F32, name="neg_a_%d" % t)
+            nc.vector.scalar_tensor_tensor(neg_a[:], banks["w2", t][:], 0.2, span(ln_at["w2", t]), ALU.subtract, ALU.min)
+            prod[t] = keep.tile([P, S], F32, name="prod_%d" % t)
+            eng = nc.gpsimd if t in POOL_PROD else nc.vector
+            eng.tensor_tensor(prod[t][:], neg_a[:], neg_p[:], ALU.mult)
+
+        def root(t):
+            nc.scalar.activation(inv_kp[t], prod[t][:], ACT.Abs_reciprocal_sqrt, bias=0.02)
+            kp = keep.tile([P, S], F32, name="kp_%d" % t)
+            nc.vector.scalar_tensor_tensor(kp[:], prod[t][:], 0.02, inv_kp[t], ALU.add, ALU.mult)
+            if t in SCALAR_GATHER:
+                window[t] = kp
+            else:
+                window[t] = keep.tile([P, S], F32, name="kp1_%d" % t)
+                if t in VECTOR_PLUS:
+                    nc.vector.tensor_scalar(window[t][:], kp[:], 1.0, None, ALU.add)
+                else:
+                    nc.scalar.activation(window[t][:], kp[:], ACT.Identity, bias=1.0)
+
+        def gather(t, c):
+            n = CHUNKS[c]
+            cols = slice(starts[c], starts[c] + n)
+            lcols = slice(starts[c] // 16, (starts[c] + n) // 16)
+            if t in SCALAR_GATHER:
+                kr = keep.tile([P, n], F32, name="kr_%d_%d" % (t, c))
+                nc.scalar.activation(kr[:], window[t][:].indirect(riv_t[:, lcols]), ACT.Copy)
+                nc.vector.scalar_tensor_tensor(ratio[c][:, t, :], kr[:], 1.0, inv_kp[t][:, cols], ALU.add, ALU.mult)
+            else:
+                nc.vector.tensor_tensor(ratio[c][:, t, :], window[t][:].indirect(riv_t[:, lcols]), inv_kp[t][:, cols], ALU.mult)
+
+        load = {}
+        mix = {}
+        hid = {}
+
+        def loading(c):
+            n = CHUNKS[c]
+            square = keep.tile([P, n, PACK], F32, name="square_%d" % c)
+            nc.scalar.activation(square[:].rearrange("p (c i) t -> p c t i", i=4), ratio[c][:].rearrange("p t (c i) -> p c t i", i=4), ACT.Square, bias=1.0)
+            load[c] = keep.tile([P, n // 2, 2, PACK], F32, name="load_%d" % c)
+            nc.scalar.activation(load[c][:].rearrange("p v d t -> p (v d t)"), square[:].rearrange("p j t -> p (j t)"), ACT.Abs_reciprocal_sqrt)
+            mix[c] = keep.tile([P, n // 2, PACK], F32, name="mix_%d" % c)
+            nc.vector.tensor_tensor(mix[c][:], load[c][:, :, 0, :], load[c][:, :, 1, :], ALU.add)
+
+        def hidden(c):
+            V = CHUNKS[c] // 2
+            mix_sq = keep.tile([P, V * PACK], F32, name="mix_sq_%d" % c)
+            nc.scalar.activation(mix_sq[:], mix[c][:].rearrange("p v t -> p (v t)"), ACT.Square, bias=0.2)
+            inv_mix = keep.tile([P, V, PACK], F32, name="inv_mix_%d" % c)
+            nc.scalar.activation(inv_mix[:].rearrange("p v t -> p (v t)"), mix_sq[:], ACT.Abs_reciprocal_sqrt)
+            factor = keep.tile([P, V, PACK], F32, name="factor_%d" % c)
+            nc.vector.scalar_tensor_tensor(factor[:], inv_mix[:], 1.0 / 0.6, gain[:].unsqueeze(1).to_broadcast([P, V, PACK]), ALU.subtract, ALU.mult)
+            hid[c] = keep.tile([P, V, 2, PACK], BF16, name="hid_%d" % c, align_bytes=64)
+            nc.vector.tensor_tensor(hid[c][:], load[c][:], factor[:].unsqueeze(2).to_broadcast([P, V, 2, PACK]), ALU.mult)
+
+        def last_product(c):
+            n = CHUNKS[c]
+            cols = slice(starts[c], starts[c] + n)
+            hid_codes = keep.tile([P, n], U32, name="hid_codes_%d" % c, align_bytes=64)
+            hid_plane = keep.tile([P, n], U8, name="hid_plane_%d" % c, align_bytes=64)
+            nc.vector.quantize_mx(hid_codes[:].bitcast(FP8X4), hid_plane[:], hid[c][:].rearrange("p v d t -> p (v d t)"))
+            acc = psum.tile([P, 2, n], F32, name="acc_%d" % c, tag="bank_%s_%d" % ("w2" if c < 4 else "w1", order[c % 4]))
+            for m in range(2):
+                mcols = slice(m * P, (m + 1) * P)
+                nc.tensor.matmul_mx(acc[:, m, :], codes_w3[:, mcols].bitcast(FP8X4), plane_w3[:, mcols],
+                                    hid_codes[:].bitcast(FP8X4), hid_plane[:], start=True, stop=True)
+            result = keep.tile([P, 2, n], F32, name="result_%d" % c)
+            nc.scalar.copy(result[:], acc[:])
+            nc.sync.dma_start(out.rearrange("(m p) j -> p m j", p=P)[:, :, cols], result[:])
+
+        nchunks = len(CHUNKS)
+        for t in order:
+            product(t)
+        for i, t in enumerate(order):
+            root(t)
+            if i > 0:
+                gather(order[i - 1], 0)
+        gather(order[3], 0)
+        for step in range(nchunks + 2):
+            if step < nchunks:
+                loading(step)
+            if step + 1 < nchunks:
+                for t in order:
+                    gather(t, step + 1)
+            if 0 <= step - 1 < nchunks:
+                hidden(step - 1)
+            if 0 <= step - 2 < nchunks:
+                last_product(step - 2)

@@ -19,9 +19,9 @@ P = 128
 PACK = 4
 CHUNKS = [128,128,128,64,64]
 FLOOR = 2.0 ** -44
-SCALAR_GATHER = [2]
-VECTOR_PLUS = []
-POOL_PROD = []
+SCALAR_GATHER = [3,2]
+VECTOR_PLUS = [0,1]
+POOL_PROD = [3,2,0]
 
 
 def tile_picked_yadsiso_load_p_kernel(tc, x_words, x_scales, w1, w2, unit, w3, offs, riv, out):
@@ -34,34 +34,37 @@ def tile_picked_yadsiso_load_p_kernel(tc, x_words, x_scales, w1, w2, unit, w3, o
         riv_t = keep.tile([P, S // 16], U16, name="riv_t")
         table_words = keep.tile([P, T], I32, name="table_words", align_bytes=64)
         table_scales = keep.tile([P, T], U8, name="table_scales", align_bytes=64)
-        nc.gpsimd.memset(table_scales[:].bitcast(I32), 0)
+        nc.vector.memset(table_scales[:, : T // 2].bitcast(I32), 0)
+        nc.gpsimd.memset(table_scales[:, T // 2 :].bitcast(I32), 0)
         half = H // 2
         raw_w2 = keep.tile([P, PACK, H], F32, name="raw_w2")
         nc.sync.dma_start(raw_w2[:], w2.rearrange("(p j) c -> p j c", j=PACK))
-        for q in range(4):
-            nc.sync.dma_start(table_scales[32 * q : 32 * q + 4, :].bitcast(I32), x_scales[0, 4 * q : 4 * q + 4, :].bitcast(I32))
         nc.sync.dma_start(offs_t[:], offs)
+        nc.sync.dma_start(riv_t[:], riv)
+        for q in range(4):
+            nc.sync.dma_start(table_scales[q:P:32, :].bitcast(I32), x_scales[0, q:16:4, :].bitcast(I32))
         nc.sync.dma_start(table_words[:], x_words[0].rearrange("p n t -> p (n t)").bitcast(I32))
         raw_w1 = []
         for h in range(2):
-            raw_w1.append(keep.tile([P, PACK, half], F32, name="raw_w1_%d" % h))
-            nc.sync.dma_start(raw_w1[h][:], w1.rearrange("(p j) c -> p j c", j=PACK)[:, :, h * half : (h + 1) * half])
+            raw_w1.append(keep.tile([P, 2, H], F32, name="raw_w1_%d" % h))
+            nc.sync.dma_start(raw_w1[h][:], w1.rearrange("(p j) c -> p j c", j=PACK)[:, 2 * h : 2 * h + 2, :])
         raw_w3 = keep.tile([P, PACK, N], F32, name="raw_w3")
         nc.sync.dma_start(raw_w3[:], w3.rearrange("(p j) c -> p j c", j=PACK))
         unit_t = keep.tile([P, PACK], F32, name="unit_t")
         nc.sync.dma_start(unit_t[:], unit.rearrange("(p t) o -> p (t o)", t=PACK))
-        nc.sync.dma_start(riv_t[:], riv)
 
         grouped = {name: keep.tile([P, PACK, P, PACK], BF16, name="grouped_" + name, align_bytes=64) for name in ("w2", "w1")}
         codes = {name: keep.tile([P, H], U32, name="codes_" + name, align_bytes=64) for name in ("w2", "w1")}
         plane = {name: keep.tile([P, H], U8, name="plane_" + name, align_bytes=64) for name in ("w2", "w1")}
 
         x_codes = [keep.tile([P, S // 2], U32, name="x_codes_%d" % h, align_bytes=64) for h in range(2)]
-        x_plane = keep.tile([P, S], U8, name="x_plane", align_bytes=64)
-        nc.vector.tensor_copy(x_plane[:], table_scales[:].indirect(offs_t[:]))
-        nc.vector.tensor_scalar(grouped["w2"][:].rearrange("p t m j -> p m j t"), raw_w2[:].rearrange("p j (m t) -> p m j t", t=PACK), -1.0, None, ALU.mult)
+        x_plane = [keep.tile([P, S // 2], U8, name="x_plane_%d" % h, align_bytes=64) for h in range(2)]
+        dst = grouped["w2"][:].rearrange("p t m j -> p m j t")
+        src = raw_w2[:].rearrange("p j (m t) -> p m j t", t=PACK)
+        nc.vector.tensor_scalar(dst, src, -1.0, None, ALU.mult)
         nc.vector.quantize_mx(codes["w2"][:].bitcast(FP8X4), plane["w2"][:], grouped["w2"][:].rearrange("p t m j -> p (t m j)"))
         for h in range(2):
+            nc.vector.tensor_copy(x_plane[h][:], table_scales[:].indirect(offs_t[:, 16 * h : 16 * (h + 1)]))
             nc.vector.tensor_copy(x_codes[h][:], table_words[:].bitcast(U32).indirect(offs_t[:, 16 * h : 16 * (h + 1)]))
 
         U = S // 2
@@ -70,27 +73,37 @@ def tile_picked_yadsiso_load_p_kernel(tc, x_words, x_scales, w1, w2, unit, w3, o
         def span(u):
             return ring[:, u * U : (u + 2) * U]
 
-        sig_at = {("w2", 0): 0, ("w2", 1): 2, ("w2", 2): 4, ("w2", 3): 6, ("w1", 0): 8, ("w1", 1): 10, ("w1", 3): 13, ("w1", 2): 17}
+        sig_at = {("w2", 0): 0, ("w2", 1): 2, ("w2", 2): 4, ("w2", 3): 6, ("w1", 0): 8, ("w1", 2): 10, ("w1", 3): 13, ("w1", 1): 17}
 
         banks = {}
 
+        def multiply(name, t, h, target):
+            cols = slice(t * P, (t + 1) * P)
+            nc.tensor.matmul_mx(target, codes[name][:, cols].bitcast(FP8X4), plane[name][:, cols],
+                                x_codes[h][:].bitcast(FP8X4), x_plane[h][:], start=True, stop=True)
+
         def first_products(name):
-            for t in range(PACK):
-                cols = slice(t * P, (t + 1) * P)
-                banks[name, t] = psum.tile([P, S], F32, name="bank_%s_%d" % (name, t), tag="bank_%s_%d" % (name, t))
-                for h in range(2):
-                    hc = slice(h * U, (h + 1) * U)
-                    nc.tensor.matmul_mx(banks[name, t][:, hc], codes[name][:, cols].bitcast(FP8X4), plane[name][:, cols],
-                                        x_codes[h][:].bitcast(FP8X4), x_plane[:, hc], start=True, stop=True)
-                nc.scalar.activation(span(sig_at[name, t]), banks[name, t][:], ACT.Sigmoid, scale=1.0 if name == "w2" else -1.0)
+            for b in ([1, 0, 3, 2] if name == "w2" else range(PACK)):
+                banks[name, b] = psum.tile([P, S], F32, name="bank_%s_%d" % (name, b), tag="bank_%s_%d" % (name, b))
+                for u in range(2):
+                    target = banks[name, b][:, u * U : (u + 1) * U]
+                    if name == "w2":
+                        multiply(name, 2 * (b % 2) + u, b // 2, target)
+                    else:
+                        multiply(name, b, u, target)
+                nc.scalar.activation(span(sig_at[name, b]), banks[name, b][:], ACT.Sigmoid, scale=1.0 if name == "w2" else -1.0)
 
         first_products("w2")
-        for h in range(2):
-            nc.vector.tensor_copy(
-                grouped["w1"][:, :, h * 64 : (h + 1) * 64, :].rearrange("p t m j -> p m j t"),
-                raw_w1[h][:].rearrange("p j (m t) -> p m j t", t=PACK),
-            )
-        for t in range(PACK):
+        nc.vector.tensor_copy(
+            grouped["w1"][:, :, :, 0:2].rearrange("p t m j -> p m j t"),
+            raw_w1[0][:].rearrange("p j (m t) -> p m j t", t=PACK),
+        )
+        for t in range(PACK + 1):
+            if t < PACK:
+                nc.vector.tensor_copy(grouped["w1"][:, t, :, 2:4], raw_w1[1][:].rearrange("p j (m t) -> p t m j", t=PACK)[:, t])
+            if t == 0:
+                continue
+            t -= 1
             cols = slice(t * P, (t + 1) * P)
             nc.vector.quantize_mx(codes["w1"][:, cols].bitcast(FP8X4), plane["w1"][:, cols], grouped["w1"][:, t].rearrange("p m j -> p (m j)"))
         first_products("w1")
@@ -103,7 +116,7 @@ def tile_picked_yadsiso_load_p_kernel(tc, x_words, x_scales, w1, w2, unit, w3, o
         plane_w3 = keep.tile([P, N], U8, name="plane_w3", align_bytes=64)
         nc.vector.quantize_mx(codes_w3[:].bitcast(FP8X4), plane_w3[:], grouped_w3[:].rearrange("p c j -> p (c j)"))
 
-        ln_order = [("w1", 3), ("w2", 3), ("w2", 0), ("w1", 0), ("w2", 1), ("w1", 1), ("w2", 2), ("w1", 2)]
+        ln_order = [("w1", 3), ("w2", 1), ("w2", 3), ("w1", 2), ("w2", 0), ("w2", 2), ("w1", 0), ("w1", 1)]
         ln_at = {ln_order[0]: 20, ln_order[1]: 12, ln_order[2]: 14}
         for i in range(3, 8):
             ln_at[ln_order[i]] = sig_at[ln_order[i - 2]]
@@ -112,7 +125,9 @@ def tile_picked_yadsiso_load_p_kernel(tc, x_words, x_scales, w1, w2, unit, w3, o
             s = shrink if key[0] == "w2" else 1.0
             nc.scalar.activation(span(ln_at[key]), span(sig_at[key]), ACT.Ln, bias=FLOOR * s, scale=s)
 
-        order = [3, 0, 1, 2]
+        order = [3, 2, 0, 1]
+        neg_a = keep.tile([P, PACK * S], F32, name="neg_a")
+        neg_a_view = neg_a[:].rearrange("p (tp u h j) -> p tp h u j", tp=2, u=2, h=2)
         prod = {}
         inv_kp = {order[0]: span(16), order[1]: span(18)}
         for t in order[2:]:
@@ -124,11 +139,15 @@ def tile_picked_yadsiso_load_p_kernel(tc, x_words, x_scales, w1, w2, unit, w3, o
         def product(t):
             neg_p = keep.tile([P, S], F32, name="neg_p_%d" % t)
             nc.vector.scalar_tensor_tensor(neg_p[:], banks["w1", t][:], -1.0, span(ln_at["w1", t]), ALU.mult, ALU.min)
-            neg_a = keep.tile([P, S], F32, name="neg_a_%d" % t)
-            nc.vector.scalar_tensor_tensor(neg_a[:], banks["w2", t][:], 0.2, span(ln_at["w2", t]), ALU.subtract, ALU.min)
+            if t in (order[0], order[2]):
+                for h in range(2):
+                    b = 2 * h + t // 2
+                    nc.vector.scalar_tensor_tensor(
+                        neg_a_view[:, t // 2, h], banks["w2", b][:].rearrange("p (u j) -> p u j", u=2), 0.2,
+                        span(ln_at["w2", b]).rearrange("p (u j) -> p u j", u=2), ALU.subtract, ALU.min)
             prod[t] = keep.tile([P, S], F32, name="prod_%d" % t)
             eng = nc.gpsimd if t in POOL_PROD else nc.vector
-            eng.tensor_tensor(prod[t][:], neg_a[:], neg_p[:], ALU.mult)
+            eng.tensor_tensor(prod[t][:], neg_a[:, t * S : (t + 1) * S], neg_p[:], ALU.mult)
 
         def root(t):
             nc.scalar.activation(inv_kp[t], prod[t][:], ACT.Abs_reciprocal_sqrt, bias=0.02)
@@ -170,9 +189,15 @@ def tile_picked_yadsiso_load_p_kernel(tc, x_words, x_scales, w1, w2, unit, w3, o
         def hidden(c):
             V = CHUNKS[c] // 2
             mix_sq = keep.tile([P, V * PACK], F32, name="mix_sq_%d" % c)
-            nc.scalar.activation(mix_sq[:], mix[c][:].rearrange("p v t -> p (v t)"), ACT.Square, bias=0.2)
+            flat = mix[c][:].rearrange("p v t -> p (v t)")
+            if c in []:
+                nc.vector.scalar_tensor_tensor(mix_sq[:], flat, 0.4, flat, ALU.add, ALU.mult)
+                rest = 0.04
+            else:
+                nc.scalar.activation(mix_sq[:], flat, ACT.Square, bias=0.2)
+                rest = 0.0
             inv_mix = keep.tile([P, V, PACK], F32, name="inv_mix_%d" % c)
-            nc.scalar.activation(inv_mix[:].rearrange("p v t -> p (v t)"), mix_sq[:], ACT.Abs_reciprocal_sqrt)
+            nc.scalar.activation(inv_mix[:].rearrange("p v t -> p (v t)"), mix_sq[:], ACT.Abs_reciprocal_sqrt, bias=rest)
             factor = keep.tile([P, V, PACK], F32, name="factor_%d" % c)
             nc.vector.scalar_tensor_tensor(factor[:], inv_mix[:], 1.0 / 0.6, gain[:].unsqueeze(1).to_broadcast([P, V, PACK]), ALU.subtract, ALU.mult)
             hid[c] = keep.tile([P, V, 2, PACK], BF16, name="hid_%d" % c, align_bytes=64)

from contextlib import ExitStack

import concourse.mybir as mybir

K, T, S, H, N = 512, 2048, 512, 512, 256
FLOPS = 2 * K * H * S * 2 + 2 * H * N * S

F32 = mybir.dt.float32
BF16 = mybir.dt.bfloat16
I32 = mybir.dt.int32
U32 = mybir.dt.uint32
U16 = mybir.dt.uint16
U8 = mybir.dt.uint8
FP8X4 = mybir.dt.float8_e4m3fn_x4
ACT = mybir.ActivationFunctionType
ALU = mybir.AluOpType

P = 128
PACK = 4
CHUNKS = [128,128,128,64,64]
FLOOR = 2.0 ** -44
SCALAR_GATHER = [3,2]
VECTOR_PLUS = [0,1]
POOL_PROD = [3,2,0]


def tile_picked_yadsiso_load_p_kernel(tc, x_words, x_scales, w1, w2, unit, w3, offs, riv, out):
    nc = tc.nc
    with ExitStack() as ctx:
        keep = ctx.enter_context(tc.tile_pool(name="keep", bufs=1))
        psum = ctx.enter_context(tc.psum_pool(name="psum", bufs=1))

        offs_t = keep.tile([P, S // 16], U16, name="offs_t")
        riv_t = keep.tile([P, S // 16], U16, name="riv_t")
        table_words = keep.tile([P, T], I32, name="table_words", align_bytes=64)
        table_scales = keep.tile([P, T], U8, name="table_scales", align_bytes=64)
        nc.vector.memset(table_scales[:, : T // 2].bitcast(I32), 0)
        nc.gpsimd.memset(table_scales[:, T // 2 :].bitcast(I32), 0)
        half = H // 2
        raw_w2 = keep.tile([P, PACK, H], F32, name="raw_w2")
        nc.sync.dma_start(raw_w2[:], w2.rearrange("(p j) c -> p j c", j=PACK))
        nc.sync.dma_start(offs_t[:], offs)
        nc.sync.dma_start(riv_t[:], riv)
        for q in range(4):
            nc.sync.dma_start(table_scales[q:P:32, :].bitcast(I32), x_scales[0, q:16:4, :].bitcast(I32))
        nc.sync.dma_start(table_words[:], x_words[0].rearrange("p n t -> p (n t)").bitcast(I32))
        raw_w1 = []
        for h in range(2):
            raw_w1.append(keep.tile([P, 2, H], F32, name="raw_w1_%d" % h))
            nc.sync.dma_start(raw_w1[h][:], w1.rearrange("(p j) c -> p j c", j=PACK)[:, 2 * h : 2 * h + 2, :])
        raw_w3 = keep.tile([P, PACK, N], F32, name="raw_w3")
        nc.sync.dma_start(raw_w3[:], w3.rearrange("(p j) c -> p j c", j=PACK))
        unit_t = keep.tile([P, PACK], F32, name="unit_t")
        nc.sync.dma_start(unit_t[:], unit.rearrange("(p t) o -> p (t o)", t=PACK))

        grouped = {name: keep.tile([P, PACK, P, PACK], BF16, name="grouped_" + name, align_bytes=64) for name in ("w2", "w1")}
        codes = {name: keep.tile([P, H], U32, name="codes_" + name, align_bytes=64) for name in ("w2", "w1")}
        plane = {name: keep.tile([P, H], U8, name="plane_" + name, align_bytes=64) for name in ("w2", "w1")}

        x_codes = [keep.tile([P, S // 2], U32, name="x_codes_%d" % h, align_bytes=64) for h in range(2)]
        x_plane = [keep.tile([P, S // 2], U8, name="x_plane_%d" % h, align_bytes=64) for h in range(2)]
        dst = grouped["w2"][:].rearrange("p t m j -> p m j t")
        src = raw_w2[:].rearrange("p j (m t) -> p m j t", t=PACK)
        nc.vector.tensor_scalar(dst, src, -1.0, None, ALU.mult)
        nc.vector.quantize_mx(codes["w2"][:].bitcast(FP8X4), plane["w2"][:], grouped["w2"][:].rearrange("p t m j -> p (t m j)"))
        for h in range(2):
            nc.vector.tensor_copy(x_plane[h][:], table_scales[:].indirect(offs_t[:, 16 * h : 16 * (h + 1)]))
            nc.vector.tensor_copy(x_codes[h][:], table_words[:].bitcast(U32).indirect(offs_t[:, 16 * h : 16 * (h + 1)]))

        U = S // 2
        ring = keep.tile([P, 22 * U], F32, name="ring")

        def span(u):
            return ring[:, u * U : (u + 2) * U]

        sig_at = {("w2", 0): 0, ("w2", 1): 2, ("w2", 2): 4, ("w2", 3): 6, ("w1", 0): 8, ("w1", 2): 10, ("w1", 3): 13, ("w1", 1): 17}

        banks = {}

        def multiply(name, t, h, target):
            cols = slice(t * P, (t + 1) * P)
            nc.tensor.matmul_mx(target, codes[name][:, cols].bitcast(FP8X4), plane[name][:, cols],
                                x_codes[h][:].bitcast(FP8X4), x_plane[h][:], start=True, stop=True)

        def first_products(name):
            for b in ([1, 0, 3, 2] if name == "w2" else range(PACK)):
                banks[name, b] = psum.tile([P, S], F32, name="bank_%s_%d" % (name, b), tag="bank_%s_%d" % (name, b))
                for u in range(2):
                    target = banks[name, b][:, u * U : (u + 1) * U]
                    if name == "w2":
                        multiply(name, 2 * (b % 2) + u, b // 2, target)
                    else:
                        multiply(name, b, u, target)
                nc.scalar.activation(span(sig_at[name, b]), banks[name, b][:], ACT.Sigmoid, scale=1.0 if name == "w2" else -1.0)

        first_products("w2")
        nc.vector.tensor_copy(
            grouped["w1"][:, :, :, 0:2].rearrange("p t m j -> p m j t"),
            raw_w1[0][:].rearrange("p j (m t) -> p m j t", t=PACK),
        )
        for t in range(PACK + 1):
            if t < PACK:
                nc.vector.tensor_copy(grouped["w1"][:, t, :, 2:4], raw_w1[1][:].rearrange("p j (m t) -> p t m j", t=PACK)[:, t])
            if t == 0:
                continue
            t -= 1
            cols = slice(t * P, (t + 1) * P)
            nc.vector.quantize_mx(codes["w1"][:, cols].bitcast(FP8X4), plane["w1"][:, cols], grouped["w1"][:, t].rearrange("p m j -> p (m j)"))
        first_products("w1")

        grouped_w3 = keep.tile([P, N, PACK], BF16, name="grouped_w3", align_bytes=64)
        nc.vector.tensor_copy(grouped_w3[:].rearrange("p (c i) j -> p c j i", i=4), raw_w3[:].rearrange("p j (c i) -> p c j i", i=4))
        gain = keep.tile([P, PACK], F32, name="gain")
        nc.vector.tensor_scalar(gain[:], unit_t[:], -0.6, None, ALU.mult)
        codes_w3 = keep.tile([P, N], U32, name="codes_w3", align_bytes=64)
        plane_w3 = keep.tile([P, N], U8, name="plane_w3", align_bytes=64)
        nc.vector.quantize_mx(codes_w3[:].bitcast(FP8X4), plane_w3[:], grouped_w3[:].rearrange("p c j -> p (c j)"))

        ln_order = [("w1", 3), ("w2", 1), ("w2", 3), ("w1", 2), ("w2", 0), ("w2", 2), ("w1", 0), ("w1", 1)]
        ln_at = {ln_order[0]: 20, ln_order[1]: 12, ln_order[2]: 14}
        for i in range(3, 8):
            ln_at[ln_order[i]] = sig_at[ln_order[i - 2]]
        shrink = 2.718281828459045 ** -0.2
        for key in ln_order:
            s = shrink if key[0] == "w2" else 1.0
            nc.scalar.activation(span(ln_at[key]), span(sig_at[key]), ACT.Ln, bias=FLOOR * s, scale=s)

        order = [3, 2, 0, 1]
        neg_a = keep.tile([P, PACK * S], F32, name="neg_a")
        neg_a_view = neg_a[:].rearrange("p (tp u h j) -> p tp h u j", tp=2, u=2, h=2)
        prod = {}
        inv_kp = {order[0]: span(16), order[1]: span(18)}
        for t in order[2:]:
            inv_kp[t] = keep.tile([P, S], F32, name="inv_kp_%d" % t)[:]
        starts = [sum(CHUNKS[:c]) for c in range(len(CHUNKS))]
        ratio = [keep.tile([P, PACK, n], F32, name="ratio_%d" % c) for c, n in enumerate(CHUNKS)]
        window = {}

        def product(t):
            neg_p = keep.tile([P, S], F32, name="neg_p_%d" % t)
            nc.vector.scalar_tensor_tensor(neg_p[:], banks["w1", t][:], -1.0, span(ln_at["w1", t]), ALU.mult, ALU.min)
            if t in (order[0], order[2]):
                for h in range(2):
                    b = 2 * h + t // 2
                    nc.vector.scalar_tensor_tensor(
                        neg_a_view[:, t // 2, h], banks["w2", b][:].rearrange("p (u j) -> p u j", u=2), 0.2,
                        span(ln_at["w2", b]).rearrange("p (u j) -> p u j", u=2), ALU.subtract, ALU.min)
            prod[t] = keep.tile([P, S], F32, name="prod_%d" % t)
            eng = nc.gpsimd if t in POOL_PROD else nc.vector
            eng.tensor_tensor(prod[t][:], neg_a[:, t * S : (t + 1) * S], neg_p[:], ALU.mult)

        def root(t):
            nc.scalar.activation(inv_kp[t], prod[t][:], ACT.Abs_reciprocal_sqrt, bias=0.02)
            kp = keep.tile([P, S], F32, name="kp_%d" % t)
            nc.vector.scalar_tensor_tensor(kp[:], prod[t][:], 0.02, inv_kp[t], ALU.add, ALU.mult)
            if t in SCALAR_GATHER:
                window[t] = kp
            else:
                window[t] = keep.tile([P, S], F32, name="kp1_%d" % t)
                if t in VECTOR_PLUS:
                    nc.vector.tensor_scalar(window[t][:], kp[:], 1.0, None, ALU.add)
                else:
                    nc.scalar.activation(window[t][:], kp[:], ACT.Identity, bias=1.0)

        def gather(t, c):
            n = CHUNKS[c]
            cols = slice(starts[c], starts[c] + n)
            lcols = slice(starts[c] // 16, (starts[c] + n) // 16)
            if t in SCALAR_GATHER:
                kr = keep.tile([P, n], F32, name="kr_%d_%d" % (t, c))
                nc.scalar.activation(kr[:], window[t][:].indirect(riv_t[:, lcols]), ACT.Copy)
                nc.vector.scalar_tensor_tensor(ratio[c][:, t, :], kr[:], 1.0, inv_kp[t][:, cols], ALU.add, ALU.mult)
            else:
                nc.vector.tensor_tensor(ratio[c][:, t, :], window[t][:].indirect(riv_t[:, lcols]), inv_kp[t][:, cols], ALU.mult)

        load = {}
        mix = {}
        hid = {}

        def loading(c):
            n = CHUNKS[c]
            square = keep.tile([P, n, PACK], F32, name="square_%d" % c)
            nc.scalar.activation(square[:].rearrange("p (c i) t -> p c t i", i=4), ratio[c][:].rearrange("p t (c i) -> p c t i", i=4), ACT.Square, bias=1.0)
            load[c] = keep.tile([P, n // 2, 2, PACK], F32, name="load_%d" % c)
            nc.scalar.activation(load[c][:].rearrange("p v d t -> p (v d t)"), square[:].rearrange("p j t -> p (j t)"), ACT.Abs_reciprocal_sqrt)
            mix[c] = keep.tile([P, n // 2, PACK], F32, name="mix_%d" % c)
            nc.vector.tensor_tensor(mix[c][:], load[c][:, :, 0, :], load[c][:, :, 1, :], ALU.add)

        def hidden(c):
            V = CHUNKS[c] // 2
            mix_sq = keep.tile([P, V * PACK], F32, name="mix_sq_%d" % c)
            flat = mix[c][:].rearrange("p v t -> p (v t)")
            if c in []:
                nc.vector.scalar_tensor_tensor(mix_sq[:], flat, 0.4, flat, ALU.add, ALU.mult)
                rest = 0.04
            else:
                nc.scalar.activation(mix_sq[:], flat, ACT.Square, bias=0.2)
                rest = 0.0
            inv_mix = keep.tile([P, V, PACK], F32, name="inv_mix_%d" % c)
            nc.scalar.activation(inv_mix[:].rearrange("p v t -> p (v t)"), mix_sq[:], ACT.Abs_reciprocal_sqrt, bias=rest)
            factor = keep.tile([P, V, PACK], F32, name="factor_%d" % c)
            nc.vector.scalar_tensor_tensor(factor[:], inv_mix[:], 1.0 / 0.6, gain[:].unsqueeze(1).to_broadcast([P, V, PACK]), ALU.subtract, ALU.mult)
            hid[c] = keep.tile([P, V, 2, PACK], BF16, name="hid_%d" % c, align_bytes=64)
            nc.vector.tensor_tensor(hid[c][:], load[c][:], factor[:].unsqueeze(2).to_broadcast([P, V, 2, PACK]), ALU.mult)

        def last_product(c):
            n = CHUNKS[c]
            cols = slice(starts[c], starts[c] + n)
            hid_codes = keep.tile([P, n], U32, name="hid_codes_%d" % c, align_bytes=64)
            hid_plane = keep.tile([P, n], U8, name="hid_plane_%d" % c, align_bytes=64)
            nc.vector.quantize_mx(hid_codes[:].bitcast(FP8X4), hid_plane[:], hid[c][:].rearrange("p v d t -> p (v d t)"))
            acc = psum.tile([P, 2, n], F32, name="acc_%d" % c, tag="bank_%s_%d" % ("w2" if c < 4 else "w1", order[c % 4]))
            for m in range(2):
                mcols = slice(m * P, (m + 1) * P)
                nc.tensor.matmul_mx(acc[:, m, :], codes_w3[:, mcols].bitcast(FP8X4), plane_w3[:, mcols],
                                    hid_codes[:].bitcast(FP8X4), hid_plane[:], start=True, stop=True)
            result = keep.tile([P, 2, n], F32, name="result_%d" % c)
            nc.scalar.copy(result[:], acc[:])
            nc.sync.dma_start(out.rearrange("(m p) j -> p m j", p=P)[:, :, cols], result[:])

        nchunks = len(CHUNKS)
        for t in order:
            product(t)
        for i, t in enumerate(order):
            root(t)
            if i > 0:
                gather(order[i - 1], 0)
        gather(order[3], 0)
        for step in range(nchunks + 2):
            if step < nchunks:
                loading(step)
            if step + 1 < nchunks:
                for t in order:
                    gather(t, step + 1)
            if 0 <= step - 1 < nchunks:
                hidden(step - 1)
            if 0 <= step - 2 < nchunks:
                last_product(step - 2)
